import numpy as np
import ml_dtypes


def mxq(x, axis, fmt="e4m3"):
    dtype, down = {"e4m3": (ml_dtypes.float8_e4m3fn, 7), "e5m2": (ml_dtypes.float8_e5m2, 14)}[fmt]
    v = np.moveaxis(np.asarray(x, np.float32).astype(ml_dtypes.bfloat16).astype(np.float64), axis, -1)
    blocks = v.reshape(v.shape[:-1] + (-1, 32))
    amax = np.abs(blocks).max(-1, keepdims=True)
    byte = np.maximum(np.where(amax > 0, np.frexp(amax)[1] - 1 + 127, 0) - down, 1)
    scale = np.exp2(byte - 127.0)
    codes = (blocks / scale).astype(np.float32).astype(dtype).astype(np.float64)
    return np.moveaxis((codes * scale).reshape(v.shape), -1, axis)


WIDE = False


def mx_kscale(k):
    if not WIDE:
        return np.ones(k)
    levels = np.array([30, -30])
    if k % 512:
        return np.exp2(np.random.permutation(np.resize(levels, k // 32))).repeat(32)
    a = np.empty((k // 512, 16))
    for p in range(k // 512):
        a[p, :8] = np.random.permutation(np.resize(levels, 8))
        for g in range(8):
            far = levels[np.abs(levels - a[p, g]) >= 10]
            a[p, g + 8] = far[np.random.randint(len(far))]
    return np.exp2(a.ravel()).repeat(32)


BF16 = ml_dtypes.bfloat16


def bf(x):
    return np.asarray(x, np.float32).astype(BF16)


def f64(x):
    return np.asarray(x).astype(np.float64)


E2M1 = np.array([0.0, 0.5, 1.0, 1.5, 2.0, 3.0, 4.0, 6.0, -0.0, -0.5, -1.0, -1.5, -2.0, -3.0, -4.0, -6.0])


def pack_weight(w, fmt):
    k, n = w.shape
    w = f64(bf(w)).reshape(k // 32, 32, n)
    amax = np.abs(w).max(1)
    if fmt in ("e4m3", "e5m2"):
        byte = np.frexp(amax)[1] - 1 + 127 - (7 if fmt == "e4m3" else 14)
    else:
        mant, ex = np.frexp(amax / 6.0)
        byte = np.where(mant > 0.5, ex, ex - 1) + 127
    byte = np.clip(np.where(amax > 0, byte, 1), 1, 254)
    scaled = (w * np.exp2(127.0 - byte)[:, None, :]).reshape(k, n).astype(np.float32)
    by_word = np.ascontiguousarray(scaled.reshape(k // 512, 128, 4, n).transpose(0, 1, 3, 2))
    if fmt in ("e4m3", "e5m2"):
        words = by_word.astype(ml_dtypes.float8_e4m3fn if fmt == "e4m3" else ml_dtypes.float8_e5m2).view(np.uint8)
    else:
        c = by_word.astype(ml_dtypes.float4_e2m1fn).view(np.uint8) & 0xF
        words = c[..., 0::2] | (c[..., 1::2] << 4)
    return np.ascontiguousarray(words), np.ascontiguousarray(byte.astype(np.uint8).reshape(k // 512, 16, n))


def unpack_weight(words, scales, fmt):
    g, p, n, _ = words.shape
    if fmt in ("e4m3", "e5m2"):
        vals = np.ascontiguousarray(words).view(ml_dtypes.float8_e4m3fn if fmt == "e4m3" else ml_dtypes.float8_e5m2).astype(np.float64)
    else:
        nib = np.empty((g, p, n, 4), np.uint8)
        nib[..., 0::2] = words & 0xF
        nib[..., 1::2] = words >> 4
        vals = E2M1[nib]
    vals = vals * np.repeat(np.exp2(scales.astype(np.float64) - 127.0), 8, axis=1)[..., None]
    return vals.transpose(0, 1, 3, 2).reshape(g * 512, n)


P, B, M, C, DOF = 1024, 2048, 1024, 1536, 5


def setup_inputs():
    s = mx_kscale(B)
    t = mx_kscale(M)
    G = np.random.standard_t(DOF, (B, P)) * s[:, None]
    G_words, G_scales = pack_weight(G, "e5m2")
    return {"g_words": G_words,
            "g_scales": G_scales,
            "readout": bf(np.random.standard_normal((B, M)) / np.sqrt(B) / s[:, None]),
            "target": bf(0.4 * np.random.standard_normal(M)),
            "mode_gain": bf((1 + 0.1 * np.random.standard_normal(M)) * t),
            "kick": bf(np.random.standard_normal((M, C)) / np.sqrt(M) / t[:, None]),
            "pulse_gain": bf(1 + 0.1 * np.random.standard_normal(P)),
            "setting": bf(np.random.standard_normal((P, C)))}


def reference(g_words, g_scales, readout, target, mode_gain, kick, pulse_gain, setting):
    G = unpack_weight(g_words, g_scales, "e5m2")
    amp = G.T @ mxq(f64(readout), 0, "e4m3")
    h = (amp - f64(target)) * f64(mode_gain)
    dk = mxq(h, 1, "e5m2") @ mxq(f64(kick), 0, "e4m3")
    return f64(setting) - f64(pulse_gain)[:, None] * dk

@@ -1,0 +1,328 @@
+from contextlib import ExitStack
+
+import concourse.mybir as mybir
+from concourse.masks import make_identity
+
+PULSES, MONITORS, MODES, CORRECTORS = 1024, 2048, 1024, 1536
+FLOPS = 2 * PULSES * MONITORS * MODES + 2 * PULSES * MODES * CORRECTORS
+
+F32 = mybir.dt.float32
+BF16 = mybir.dt.bfloat16
+U32 = mybir.dt.uint32
+I32 = mybir.dt.int32
+U8 = mybir.dt.uint8
+E4M3 = mybir.dt.float8_e4m3fn_x4
+E5M2 = mybir.dt.float8_e5m2_x4
+ADD = mybir.AluOpType.add
+MULT = mybir.AluOpType.mult
+SUB = mybir.AluOpType.subtract
+COPY = mybir.ActivationFunctionType.Copy
+IDENTITY = mybir.ActivationFunctionType.Identity
+
+P = 128
+J = 4
+W = 512
+GROUPS = MONITORS // W
+KGROUPS = MODES // W
+HALVES = PULSES // W
+CTILES = CORRECTORS // W
+PTILES = PULSES // P
+
+
+def tile_factored_orbit_correction_e3_kernel(
+    tc, g_words, g_scales, readout, target, mode_gain, kick, pulse_gain, setting, out
+):
+    nc = tc.nc
+    with ExitStack() as ctx:
+        keep = ctx.enter_context(tc.tile_pool(name="keep", bufs=1))
+        raws = ctx.enter_context(tc.tile_pool(name="raws", bufs=3))
+        grouped_pool = ctx.enter_context(tc.tile_pool(name="grouped", bufs=6))
+        outs = ctx.enter_context(tc.tile_pool(name="outs", bufs=10))
+        psum = ctx.enter_context(tc.psum_pool(name="psum", bufs=8))
+        ctx.enter_context(tc.manual_schedule())
+
+        def kept(name, shape, dtype):
+            return keep.tile(shape, dtype, name=name, tag=name, align_bytes=64)
+
+        def bank(name):
+            return psum.tile([P, W], F32, name=name, tag="bank")
+
+        pg_rows = kept("pg_rows", [P, P], BF16)
+        ident = kept("ident", [P, P], BF16)
+        nc.gpsimd.memset(pg_rows[:], 0.0)
+        nc.gpsimd.dma_start(out=pg_rows[0:PTILES, :], in_=pulse_gain.rearrange("(i p) -> i p", p=P))
+        make_identity(nc, ident[:])
+
+        g_sc = kept("g_sc", [P, GROUPS, PULSES], U8)
+        nc.vector.memset(g_sc[:].rearrange("p g n -> p (g n)").bitcast(I32), 0)
+
+        def ro_rows(g):
+            return readout[W * g : W * (g + 1), :].rearrange("(p j) w -> p j w", j=J)
+
+        ro_raw = {}
+        g_w = {}
+        for mg in range(KGROUPS):
+            raw = kept(f"ro0_{mg}", [P, J, W], BF16)
+            nc.sync.dma_start(out=raw[:], in_=ro_rows(0)[:, :, W * mg : W * (mg + 1)])
+            ro_raw[0, mg] = raw[:]
+        for q in range(4):
+            nc.sync.dma_start(
+                out=g_sc[32 * q : 32 * q + 4].bitcast(I32),
+                in_=g_scales[:, 4 * q : 4 * q + 4, :].rearrange("g r n -> r g n").bitcast(I32),
+            )
+
+        def load_g_words(g):
+            words = kept(f"gw_{g}", [P, W], U32)
+            nc.sync.dma_start(
+                out=words[:].bitcast(I32),
+                in_=g_words[g, :, 0:W, :].rearrange("p n t -> p (n t)").bitcast(I32),
+            )
+            g_w[g, 0] = words[:]
+
+        vecs = [kept("tgt", [P, KGROUPS, J], BF16), kept("gain", [P, KGROUPS, J], BF16)]
+        tgt, gain, nbias = (kept(n, [P, KGROUPS, J], F32) for n in ("tgt32", "gain32", "nbias"))
+
+        def mode_vectors():
+            for tile, src in zip(vecs, (target, mode_gain)):
+                nc.sync.dma_start(out=tile[:], in_=src.rearrange("(g p t) -> p g t", p=P, t=J))
+            nc.gpsimd.tensor_copy(out=tgt[:], in_=vecs[0][:])
+            nc.gpsimd.tensor_copy(out=gain[:], in_=vecs[1][:])
+            nc.gpsimd.tensor_scalar(out=nbias[:], in0=tgt[:], scalar1=-1.0, scalar2=0.0, op0=MULT, op1=ADD)
+            nc.gpsimd.tensor_tensor(out=nbias[:], in0=nbias[:], in1=gain[:], op=MULT)
+
+        load_g_words(0)
+        for g in range(1, GROUPS):
+            raw = raws.tile([P, J, MODES], BF16, name="ro_raw", tag="ro_raw", align_bytes=64)
+            nc.sync.dma_start(out=raw[:], in_=ro_rows(g))
+            for mg in range(KGROUPS):
+                ro_raw[g, mg] = raw[:, :, W * mg : W * (mg + 1)]
+            if g == 1:
+                mode_vectors()
+            load_g_words(g)
+        words1 = kept("gw_half1", [P, GROUPS, W], U32)
+        nc.sync.dma_start(
+            out=words1[:].bitcast(I32),
+            in_=g_words[:, :, W : 2 * W, :].rearrange("g p n t -> p g (n t)").bitcast(I32),
+        )
+        for g in range(GROUPS):
+            g_w[g, 1] = words1[:, g, :]
+        k_raw = []
+        for g in range(KGROUPS):
+            raw = kept(f"k_raw{g}", [P, J, CORRECTORS], BF16)
+            nc.sync.dma_start(out=raw[:], in_=kick[W * g : W * (g + 1), :].rearrange("(p j) n -> p j n", j=J))
+            k_raw.append(raw)
+        sets = []
+        for i in range(PTILES):
+            st = kept(f"set{i}", [P, CORRECTORS], BF16)
+            nc.sync.dma_start(out=st[:], in_=setting[P * i : P * (i + 1), :])
+            sets.append(st)
+
+        npg = kept("npg", [P, PTILES], F32)
+
+        def pulse_gains():
+            pgt = psum.tile([P, P], BF16, name="pgt", tag="bank")
+            nc.tensor.transpose(pgt[:], pg_rows[:], ident[:])
+            nc.vector.tensor_scalar(out=npg[:], in0=pgt[:, 0:PTILES], scalar1=-1.0, scalar2=0.0, op0=MULT, op1=ADD)
+
+        ro_g, ro_c, ro_s = {}, {}, {}
+        k_g, k_c, k_s = {}, {}, {}
+        h_b, h_g, h_c, h_s = {}, {}, {}, {}
+        amp, dk, res = {}, {}, {}
+
+        def grouped():
+            return grouped_pool.tile([P, J * W], BF16, name="grp", tag="grp", align_bytes=64)
+
+        def copy_on(eng, dst, src):
+            if eng == "V":
+                nc.vector.tensor_copy(out=dst, in_=src)
+            else:
+                nc.scalar.copy(out=dst, in_=src)
+
+        def quantise(name, fmt, src):
+            codes = kept(name + "_c", [P, W], U32)
+            scales = kept(name + "_s", [P, W], U8)
+            nc.vector.quantize_mx(out=codes[:].bitcast(fmt), scales=scales[:], in_=src[:])
+            return codes, scales
+
+        def IR(eng, g, mg):
+            ro_g[g, mg] = grouped()
+            copy_on(
+                eng,
+                ro_g[g, mg][:].rearrange("p (t m j) -> p m j t", t=J, j=J),
+                ro_raw[g, mg].rearrange("p j (m t) -> p m j t", t=J),
+            )
+
+        def QR(g, mg):
+            ro_c[g, mg], ro_s[g, mg] = quantise(f"ro{g}{mg}", E4M3, ro_g[g, mg])
+
+        def P1(h, mt, g):
+            if g == 0:
+                amp[h, mt] = bank(f"amp{h}{mt}")
+            mg, t = divmod(mt, J)
+            cols = slice(P * t, P * (t + 1))
+            nc.tensor.matmul_mx(
+                out=amp[h, mt][:],
+                lhsT=ro_c[g, mg][:, cols].bitcast(E4M3),
+                lhsT_scale=ro_s[g, mg][:, cols],
+                rhs=g_w[g, h].bitcast(E5M2),
+                rhs_scale=g_sc[:, g, W * h : W * (h + 1)],
+                start=(g == 0),
+                stop=(g == GROUPS - 1),
+            )
+
+        def DH(eng, h, mt):
+            mg, t = divmod(mt, J)
+            if (h, mg) not in h_b:
+                h_b[h, mg] = kept(f"h{h}{mg}", [P, J, W], BF16)
+            dst = h_b[h, mg][:, t, :]
+            if eng == "V":
+                nc.vector.tensor_scalar(
+                    out=dst, in0=amp[h, mt][:], scalar1=tgt[:, mg, t : t + 1],
+                    scalar2=gain[:, mg, t : t + 1], op0=SUB, op1=MULT,
+                )
+            else:
+                nc.scalar.activation(
+                    out=dst, in_=amp[h, mt][:], func=IDENTITY,
+                    scale=gain[:, mg, t : t + 1], bias=nbias[:, mg, t : t + 1],
+                )
+
+        def interleave(eng, dst, src):
+            copy_on(
+                eng,
+                dst[:].rearrange("p (c i t) -> p c t i", i=4, t=J),
+                src.rearrange("p t (c i) -> p c t i", i=4),
+            )
+
+        def IH(eng, h, mg):
+            h_g[h, mg] = grouped()
+            interleave(eng, h_g[h, mg], h_b[h, mg][:])
+
+        def QH(h, mg):
+            h_c[h, mg], h_s[h, mg] = quantise(f"h{h}{mg}q", E5M2, h_g[h, mg])
+
+        def IK(eng, g, c):
+            k_g[g, c] = grouped()
+            interleave(eng, k_g[g, c], k_raw[g][:, :, W * c : W * (c + 1)])
+
+        def QK(g, c):
+            k_c[g, c], k_s[g, c] = quantise(f"k{g}{c}", E4M3, k_g[g, c])
+
+        def P2(i, c):
+            dk[i, c] = bank(f"dk{i}{c}")
+            h, r = divmod(i, W // P)
+            cols = slice(P * r, P * (r + 1))
+            for g in range(KGROUPS):
+                nc.tensor.matmul_mx(
+                    out=dk[i, c][:],
+                    lhsT=h_c[h, g][:, cols].bitcast(E5M2),
+                    lhsT_scale=h_s[h, g][:, cols],
+                    rhs=k_c[g, c][:].bitcast(E4M3),
+                    rhs_scale=k_s[g, c][:],
+                    start=(g == 0),
+                    stop=(g == KGROUPS - 1),
+                )
+
+        def OV(i, c):
+            res[i, c] = outs.tile([P, W], F32, name="res", tag="res", align_bytes=64)
+            nc.vector.scalar_tensor_tensor(
+                out=res[i, c][:], in0=dk[i, c][:], scalar=npg[:, i : i + 1],
+                in1=sets[i][:, W * c : W * (c + 1)], op0=MULT, op1=ADD,
+            )
+
+        def OS(i, c):
+            res[i, c] = outs.tile([P, W], F32, name="res", tag="res", align_bytes=64)
+            nc.scalar.activation(out=res[i, c][:], in_=dk[i, c][:], func=COPY, scale=npg[:, i : i + 1])
+            nc.gpsimd.tensor_tensor(
+                out=res[i, c][:], in0=res[i, c][:], in1=sets[i][:, W * c : W * (c + 1)], op=ADD
+            )
+
+        def ST(i, c):
+            nc.sync.dma_start(out=out[P * i : P * (i + 1), W * c : W * (c + 1)], in_=res[i, c][:])
+
+        def p1s(g, mg):
+            for t in range(J):
+                P1(0, J * mg + t, g)
+
+        for g in range(GROUPS):
+            IR("S" if g == 0 else "V", g, 0)
+            IR("V" if g == 0 else "S", g, 1)
+            if g:
+                QR(g - 1, 1)
+                p1s(g - 1, 1)
+            QR(g, 0)
+            p1s(g, 0)
+        QR(3, 1)
+        p1s(3, 1)
+        for mt in (0, 2, 4, 5, 6, 7):
+            DH("S", 0, mt)
+        DH("V", 0, 1)
+        DH("V", 0, 3)
+        for mt in range(8):
+            for g in range(GROUPS):
+                P1(1, mt, g)
+        IH("V", 0, 0)
+        IH("S", 0, 1)
+        DH("V", 1, 0)
+        IK("V", 0, 0)
+        QK(0, 0)
+        DH("S", 1, 1)
+        DH("S", 1, 2)
+        IK("S", 1, 0)
+        QH(0, 0)
+        IK("V", 1, 1)
+        QH(0, 1)
+        DH("S", 1, 3)
+        DH("S", 1, 4)
+        DH("V", 1, 5)
+        QK(1, 0)
+        DH("V", 1, 6)
+        QK(1, 1)
+        DH("V", 1, 7)
+        IH("S", 1, 0)
+        IH("V", 1, 1)
+        pulse_gains()
+        for i in range(4):
+            P2(i, 0)
+        OV(0, 0)
+        QH(1, 1)
+        OV(1, 0)
+        QH(1, 0)
+        OS(2, 0)
+        OS(3, 0)
+        IK("V", 0, 1)
+        for i in range(4, 8):
+            P2(i, 0)
+        OV(4, 0)
+        QK(0, 1)
+        IK("S", 1, 2)
+        OV(5, 0)
+        OV(6, 0)
+        OV(7, 0)
+        for i in range(4):
+            P2(i, 1)
+        for i in range(8):
+            ST(i, 0)
+        OV(0, 1)
+        QK(1, 2)
+        IK("S", 0, 2)
+        for i in range(1, 4):
+            OV(i, 1)
+        for i in range(4, 8):
+            P2(i, 1)
+        OV(4, 1)
+        OV(5, 1)
+        QK(0, 2)
+        OS(6, 1)
+        OV(7, 1)
+        for i in range(4):
+            P2(i, 2)
+        for i in range(8):
+            ST(i, 1)
+        for i in range(4):
+            (OV, OS, OV, OV)[i](i, 2)
+        for i in range(4, 8):
+            P2(i, 2)
+        for i in range(4, 8):
+            (OV, OS, OV, OV)[i - 4](i, 2)
+        for i in range(8):
+            ST(i, 2)

@@ -53,8 +53,18 @@ def tile_factored_orbit_correction_e3_kernel(
         nc.gpsimd.dma_start(out=pg_rows[0:PTILES, :], in_=pulse_gain.rearrange("(i p) -> i p", p=P))
         make_identity(nc, ident[:])
 
-        g_sc = kept("g_sc", [P, GROUPS, PULSES], U8)
-        nc.vector.memset(g_sc[:].rearrange("p g n -> p (g n)").bitcast(I32), 0)
+        g_sc = []
+        for h in range(HALVES):
+            plane = kept(f"g_sc{h}", [P, GROUPS, W], U8)
+            nc.vector.memset(plane[:].rearrange("p g n -> p (g n)").bitcast(I32), 0)
+            g_sc.append(plane)
+
+        def load_g_scales(h):
+            for q in range(4):
+                nc.sync.dma_start(
+                    out=g_sc[h][32 * q : 32 * q + 4].bitcast(I32),
+                    in_=g_scales[:, 4 * q : 4 * q + 4, W * h : W * (h + 1)].rearrange("g r n -> r g n").bitcast(I32),
+                )
 
         def ro_rows(g):
             return readout[W * g : W * (g + 1), :].rearrange("(p j) w -> p j w", j=J)
@@ -65,11 +75,7 @@ def tile_factored_orbit_correction_e3_kernel(
             raw = kept(f"ro0_{mg}", [P, J, W], BF16)
             nc.sync.dma_start(out=raw[:], in_=ro_rows(0)[:, :, W * mg : W * (mg + 1)])
             ro_raw[0, mg] = raw[:]
-        for q in range(4):
-            nc.sync.dma_start(
-                out=g_sc[32 * q : 32 * q + 4].bitcast(I32),
-                in_=g_scales[:, 4 * q : 4 * q + 4, :].rearrange("g r n -> r g n").bitcast(I32),
-            )
+        load_g_scales(0)
 
         def load_g_words(g):
             words = kept(f"gw_{g}", [P, W], U32)
@@ -99,6 +105,15 @@ def tile_factored_orbit_correction_e3_kernel(
             if g == 1:
                 mode_vectors()
             load_g_words(g)
+        def kick_rows(g, c0, c1):
+            return kick[W * g : W * (g + 1), W * c0 : W * c1].rearrange("(p j) n -> p j n", j=J)
+
+        k_raw = {}
+        for g in range(KGROUPS):
+            raw = kept(f"k_raw{g}0", [P, J, W], BF16)
+            nc.sync.dma_start(out=raw[:], in_=kick_rows(g, 0, 1))
+            k_raw[g, 0] = raw[:]
+        load_g_scales(1)
         words1 = kept("gw_half1", [P, GROUPS, W], U32)
         nc.sync.dma_start(
             out=words1[:].bitcast(I32),
@@ -106,11 +121,11 @@ def tile_factored_orbit_correction_e3_kernel(
         )
         for g in range(GROUPS):
             g_w[g, 1] = words1[:, g, :]
-        k_raw = []
         for g in range(KGROUPS):
-            raw = kept(f"k_raw{g}", [P, J, CORRECTORS], BF16)
-            nc.sync.dma_start(out=raw[:], in_=kick[W * g : W * (g + 1), :].rearrange("(p j) n -> p j n", j=J))
-            k_raw.append(raw)
+            raw = kept(f"k_raw{g}r", [P, J, 2 * W], BF16)
+            nc.sync.dma_start(out=raw[:], in_=kick_rows(g, 1, CTILES))
+            for c in range(1, CTILES):
+                k_raw[g, c] = raw[:, :, W * (c - 1) : W * c]
         sets = []
         for i in range(PTILES):
             st = kept(f"set{i}", [P, CORRECTORS], BF16)
@@ -165,7 +180,7 @@ def tile_factored_orbit_correction_e3_kernel(
                 lhsT=ro_c[g, mg][:, cols].bitcast(E4M3),
                 lhsT_scale=ro_s[g, mg][:, cols],
                 rhs=g_w[g, h].bitcast(E5M2),
-                rhs_scale=g_sc[:, g, W * h : W * (h + 1)],
+                rhs_scale=g_sc[h][:, g, :],
                 start=(g == 0),
                 stop=(g == GROUPS - 1),
             )
@@ -202,7 +217,7 @@ def tile_factored_orbit_correction_e3_kernel(
 
         def IK(eng, g, c):
             k_g[g, c] = grouped()
-            interleave(eng, k_g[g, c], k_raw[g][:, :, W * c : W * (c + 1)])
+            interleave(eng, k_g[g, c], k_raw[g, c])
 
         def QK(g, c):
             k_c[g, c], k_s[g, c] = quantise(f"k{g}{c}", E4M3, k_g[g, c])
@@ -243,9 +258,9 @@ def tile_factored_orbit_correction_e3_kernel(
             for t in range(J):
                 P1(0, J * mg + t, g)
 
-        for g in range(GROUPS):
-            IR("S" if g == 0 else "V", g, 0)
-            IR("V" if g == 0 else "S", g, 1)
+        for g in range(4):
+            IR("V", g, 0)
+            IR("S", g, 1)
             if g:
                 QR(g - 1, 1)
                 p1s(g - 1, 1)
@@ -253,76 +268,63 @@ def tile_factored_orbit_correction_e3_kernel(
             p1s(g, 0)
         QR(3, 1)
         p1s(3, 1)
-        for mt in (0, 2, 4, 5, 6, 7):
-            DH("S", 0, mt)
-        DH("V", 0, 1)
-        DH("V", 0, 3)
+        IK("S", 0, 0)
         for mt in range(8):
-            for g in range(GROUPS):
+            DH("VS"[mt % 2], 0, mt)
+        for mt in range(8):
+            for g in range(4):
                 P1(1, mt, g)
-        IH("V", 0, 0)
-        IH("S", 0, 1)
-        DH("V", 1, 0)
-        IK("V", 0, 0)
+        IK("V", 1, 0)
         QK(0, 0)
+        IH("S", 0, 1)
+        IH("V", 0, 0)
+        QK(1, 0)
+        DH("V", 1, 0)
+        QH(0, 1)
         DH("S", 1, 1)
         DH("S", 1, 2)
-        IK("S", 1, 0)
         QH(0, 0)
+        IK("S", 0, 1)
+        DH("V", 1, 3)
         IK("V", 1, 1)
-        QH(0, 1)
-        DH("S", 1, 3)
-        DH("S", 1, 4)
+        DH("V", 1, 4)
         DH("V", 1, 5)
-        QK(1, 0)
-        DH("V", 1, 6)
         QK(1, 1)
-        DH("V", 1, 7)
-        IH("S", 1, 0)
-        IH("V", 1, 1)
+        IH("V", 1, 0)
+        DH("S", 1, 6)
+        DH("S", 1, 7)
+        QK(0, 1)
+        IH("S", 1, 1)
         pulse_gains()
         for i in range(4):
             P2(i, 0)
+        IK("S", 1, 2)
+        IK("S", 0, 2)
         OV(0, 0)
-        QH(1, 1)
-        OV(1, 0)
         QH(1, 0)
-        OS(2, 0)
-        OS(3, 0)
-        IK("V", 0, 1)
+        OV(1, 0)
+        OV(2, 0)
+        OV(3, 0)
+        for i in range(4):
+            P2(i, 1)
+        QH(1, 1)
+        for i in range(4): OV(i, 1)
+        for i in range(4): ST(i, 0)
+        QK(1, 2)
         for i in range(4, 8):
             P2(i, 0)
-        OV(4, 0)
-        QK(0, 1)
-        IK("S", 1, 2)
-        OV(5, 0)
-        OV(6, 0)
-        OV(7, 0)
-        for i in range(4):
-            P2(i, 1)
-        for i in range(8):
-            ST(i, 0)
-        OV(0, 1)
-        QK(1, 2)
-        IK("S", 0, 2)
-        for i in range(1, 4):
-            OV(i, 1)
-        for i in range(4, 8):
-            P2(i, 1)
-        OV(4, 1)
-        OV(5, 1)
+        for i in range(4): ST(i, 1)
+        for i in range(4, 6):
+            OV(i, 0)
         QK(0, 2)
-        OS(6, 1)
-        OV(7, 1)
-        for i in range(4):
+        OV(6,0)
+        OS(7,0)
+        for i in range(4, 8):
+            P2(i, 1)
+        for i in range(4): (OV,OS)[i%2](4+i, 1)
+        for i in range(4,8): ST(i, 0)
+        for i in range(4,8): ST(i, 1)
+        for i in range(8):
             P2(i, 2)
         for i in range(8):
-            ST(i, 1)
-        for i in range(4):
-            (OV, OS, OV, OV)[i](i, 2)
-        for i in range(4, 8):
-            P2(i, 2)
-        for i in range(4, 8):
-            (OV, OS, OV, OV)[i - 4](i, 2)
-        for i in range(8):
-            ST(i, 2)
+            (OS if i in (1,3,5) else OV)(i, 2); ST(i, 2)

@@ -163,8 +163,8 @@ def tile_factored_orbit_correction_e3_kernel(
             ro_g[g, mg] = grouped()
             copy_on(
                 eng,
-                ro_g[g, mg][:].rearrange("p (t m j) -> p m j t", t=J, j=J),
-                ro_raw[g, mg].rearrange("p j (m t) -> p m j t", t=J),
+                ro_g[g, mg][:].rearrange("p (t m j) -> p m t j", t=J, j=J),
+                ro_raw[g, mg].rearrange("p j (m t) -> p m t j", t=J),
             )
 
         def QR(g, mg):

@@ -1,7 +1,6 @@
 from contextlib import ExitStack
 
 import concourse.mybir as mybir
-from concourse.masks import make_identity
 
 PULSES, MONITORS, MODES, CORRECTORS = 1024, 2048, 1024, 1536
 FLOPS = 2 * PULSES * MONITORS * MODES + 2 * PULSES * MODES * CORRECTORS
@@ -26,7 +25,6 @@ GROUPS = MONITORS // W
 KGROUPS = MODES // W
 HALVES = PULSES // W
 CTILES = CORRECTORS // W
-PTILES = PULSES // P
 
 
 def tile_factored_orbit_correction_e3_kernel(
@@ -37,7 +35,7 @@ def tile_factored_orbit_correction_e3_kernel(
         keep = ctx.enter_context(tc.tile_pool(name="keep", bufs=1))
         raws = ctx.enter_context(tc.tile_pool(name="raws", bufs=3))
         grouped_pool = ctx.enter_context(tc.tile_pool(name="grouped", bufs=6))
-        outs = ctx.enter_context(tc.tile_pool(name="outs", bufs=10))
+        outs = ctx.enter_context(tc.tile_pool(name="outs", bufs=12))
         psum = ctx.enter_context(tc.psum_pool(name="psum", bufs=8))
         ctx.enter_context(tc.manual_schedule())
 
@@ -47,11 +45,12 @@ def tile_factored_orbit_correction_e3_kernel(
         def bank(name):
             return psum.tile([P, W], F32, name=name, tag="bank")
 
-        pg_rows = kept("pg_rows", [P, P], BF16)
-        ident = kept("ident", [P, P], BF16)
-        nc.gpsimd.memset(pg_rows[:], 0.0)
-        nc.gpsimd.dma_start(out=pg_rows[0:PTILES, :], in_=pulse_gain.rearrange("(i p) -> i p", p=P))
-        make_identity(nc, ident[:])
+        def four_to_a_partition(vector):
+            return vector.rearrange("(g p t) -> p g t", p=P, t=J)
+
+        tgt_raw, gain_raw, pg_raw = (kept(n, [P, 2, J], BF16) for n in ("tgt_raw", "gain_raw", "pg_raw"))
+        tgt, gain, nbias, npg = (kept(n, [P, 2, J], F32) for n in ("tgt", "gain", "nbias", "npg"))
+        nc.gpsimd.dma_start(out=pg_raw[:], in_=four_to_a_partition(pulse_gain))
 
         g_sc = []
         for h in range(HALVES):
@@ -85,16 +84,14 @@ def tile_factored_orbit_correction_e3_kernel(
             )
             g_w[g, 0] = words[:]
 
-        vecs = [kept("tgt", [P, KGROUPS, J], BF16), kept("gain", [P, KGROUPS, J], BF16)]
-        tgt, gain, nbias = (kept(n, [P, KGROUPS, J], F32) for n in ("tgt32", "gain32", "nbias"))
-
         def mode_vectors():
-            for tile, src in zip(vecs, (target, mode_gain)):
-                nc.sync.dma_start(out=tile[:], in_=src.rearrange("(g p t) -> p g t", p=P, t=J))
-            nc.gpsimd.tensor_copy(out=tgt[:], in_=vecs[0][:])
-            nc.gpsimd.tensor_copy(out=gain[:], in_=vecs[1][:])
+            nc.sync.dma_start(out=tgt_raw[:], in_=four_to_a_partition(target))
+            nc.sync.dma_start(out=gain_raw[:], in_=four_to_a_partition(mode_gain))
+            nc.gpsimd.tensor_copy(out=tgt[:], in_=tgt_raw[:])
+            nc.gpsimd.tensor_copy(out=gain[:], in_=gain_raw[:])
             nc.gpsimd.tensor_scalar(out=nbias[:], in0=tgt[:], scalar1=-1.0, scalar2=0.0, op0=MULT, op1=ADD)
             nc.gpsimd.tensor_tensor(out=nbias[:], in0=nbias[:], in1=gain[:], op=MULT)
+            nc.gpsimd.tensor_scalar(out=npg[:], in0=pg_raw[:], scalar1=-1.0, scalar2=0.0, op0=MULT, op1=ADD)
 
         load_g_words(0)
         for g in range(1, GROUPS):
@@ -104,7 +101,9 @@ def tile_factored_orbit_correction_e3_kernel(
                 ro_raw[g, mg] = raw[:, :, W * mg : W * (mg + 1)]
             if g == 1:
                 mode_vectors()
-            load_g_words(g)
+            else:
+                load_g_words(g - 1)
+        load_g_words(GROUPS - 1)
         def kick_rows(g, c0, c1):
             return kick[W * g : W * (g + 1), W * c0 : W * c1].rearrange("(p j) n -> p j n", j=J)
 
@@ -126,18 +125,14 @@ def tile_factored_orbit_correction_e3_kernel(
             nc.sync.dma_start(out=raw[:], in_=kick_rows(g, 1, CTILES))
             for c in range(1, CTILES):
                 k_raw[g, c] = raw[:, :, W * (c - 1) : W * c]
+        def pulse_rows(array, h):
+            return array[W * h : W * (h + 1), :].rearrange("(p i) c -> p i c", i=J)
+
         sets = []
-        for i in range(PTILES):
-            st = kept(f"set{i}", [P, CORRECTORS], BF16)
-            nc.sync.dma_start(out=st[:], in_=setting[P * i : P * (i + 1), :])
+        for h in range(HALVES):
+            st = kept(f"set{h}", [P, J, CORRECTORS], BF16)
+            nc.sync.dma_start(out=st[:], in_=pulse_rows(setting, h))
             sets.append(st)
-
-        npg = kept("npg", [P, PTILES], F32)
-
-        def pulse_gains():
-            pgt = psum.tile([P, P], BF16, name="pgt", tag="bank")
-            nc.tensor.transpose(pgt[:], pg_rows[:], ident[:])
-            nc.vector.tensor_scalar(out=npg[:], in0=pgt[:, 0:PTILES], scalar1=-1.0, scalar2=0.0, op0=MULT, op1=ADD)
 
         ro_g, ro_c, ro_s = {}, {}, {}
         k_g, k_c, k_s = {}, {}, {}
@@ -159,13 +154,16 @@ def tile_factored_orbit_correction_e3_kernel(
             nc.vector.quantize_mx(out=codes[:].bitcast(fmt), scales=scales[:], in_=src[:])
             return codes, scales
 
-        def IR(eng, g, mg):
-            ro_g[g, mg] = grouped()
+        def deal(eng, dst, src):
             copy_on(
                 eng,
-                ro_g[g, mg][:].rearrange("p (t m j) -> p m t j", t=J, j=J),
-                ro_raw[g, mg].rearrange("p j (m t) -> p m t j", t=J),
+                dst[:].rearrange("p (s m r) -> p m s r", s=4, r=J),
+                src.rearrange("p r (m s) -> p m s r", s=4),
             )
+
+        def IR(eng, g, mg):
+            ro_g[g, mg] = grouped()
+            deal(eng, ro_g[g, mg], ro_raw[g, mg])
 
         def QR(g, mg):
             ro_c[g, mg], ro_s[g, mg] = quantise(f"ro{g}{mg}", E4M3, ro_g[g, mg])
@@ -210,7 +208,7 @@ def tile_factored_orbit_correction_e3_kernel(
 
         def IH(eng, h, mg):
             h_g[h, mg] = grouped()
-            interleave(eng, h_g[h, mg], h_b[h, mg][:])
+            deal(eng, h_g[h, mg], h_b[h, mg][:])
 
         def QH(h, mg):
             h_c[h, mg], h_s[h, mg] = quantise(f"h{h}{mg}q", E5M2, h_g[h, mg])
@@ -240,19 +238,19 @@ def tile_factored_orbit_correction_e3_kernel(
         def OV(i, c):
             res[i, c] = outs.tile([P, W], F32, name="res", tag="res", align_bytes=64)
             nc.vector.scalar_tensor_tensor(
-                out=res[i, c][:], in0=dk[i, c][:], scalar=npg[:, i : i + 1],
-                in1=sets[i][:, W * c : W * (c + 1)], op0=MULT, op1=ADD,
+                out=res[i, c][:], in0=dk[i, c][:], scalar=npg[:, i // J, i % J : i % J + 1],
+                in1=sets[i // J][:, i % J, W * c : W * (c + 1)], op0=MULT, op1=ADD,
             )
 
         def OS(i, c):
             res[i, c] = outs.tile([P, W], F32, name="res", tag="res", align_bytes=64)
-            nc.scalar.activation(out=res[i, c][:], in_=dk[i, c][:], func=COPY, scale=npg[:, i : i + 1])
+            nc.scalar.activation(out=res[i, c][:], in_=dk[i, c][:], func=COPY, scale=npg[:, i // J, i % J : i % J + 1])
             nc.gpsimd.tensor_tensor(
-                out=res[i, c][:], in0=res[i, c][:], in1=sets[i][:, W * c : W * (c + 1)], op=ADD
+                out=res[i, c][:], in0=res[i, c][:], in1=sets[i // J][:, i % J, W * c : W * (c + 1)], op=ADD
             )
 
         def ST(i, c):
-            nc.sync.dma_start(out=out[P * i : P * (i + 1), W * c : W * (c + 1)], in_=res[i, c][:])
+            nc.sync.dma_start(out=pulse_rows(out, i // J)[:, i % J, W * c : W * (c + 1)], in_=res[i, c][:])
 
         def p1s(g, mg):
             for t in range(J):
@@ -269,62 +267,63 @@ def tile_factored_orbit_correction_e3_kernel(
         QR(3, 1)
         p1s(3, 1)
         IK("S", 0, 0)
-        for mt in range(8):
-            DH("VS"[mt % 2], 0, mt)
-        for mt in range(8):
+        IK("V", 1, 0)
+        for mt in (0, 3, 5, 7, 6, 4):
+            DH("S", 0, mt)
+        DH("V", 0, 2)
+        QK(0, 0)
+        DH("V", 0, 1)
+        for mt in (4, 5, 6, 7, 0, 2, 3):
             for g in range(4):
                 P1(1, mt, g)
-        IK("V", 1, 0)
-        QK(0, 0)
-        IH("S", 0, 1)
-        IH("V", 0, 0)
         QK(1, 0)
-        DH("V", 1, 0)
-        QH(0, 1)
-        DH("S", 1, 1)
-        DH("S", 1, 2)
+        IH("V", 0, 0)
+        IH("V", 0, 1)
+        DH("S", 1, 4)
         QH(0, 0)
+        QH(0, 1)
         IK("S", 0, 1)
-        DH("V", 1, 3)
         IK("V", 1, 1)
-        DH("V", 1, 4)
-        DH("V", 1, 5)
-        QK(1, 1)
-        IH("V", 1, 0)
         DH("S", 1, 6)
-        DH("S", 1, 7)
+        DH("V", 1, 5)
+        for i in range(3):
+            P2(i, 0)
         QK(0, 1)
-        IH("S", 1, 1)
-        pulse_gains()
-        for i in range(4):
-            P2(i, 0)
+        QK(1, 1)
+        P2(0, 1)
         IK("S", 1, 2)
-        IK("S", 0, 2)
-        OV(0, 0)
-        QH(1, 0)
+        IK("V", 0, 2)
+        DH("S", 1, 7)
+        for g in range(4): P1(1, 1, g)
+        OS(0, 0)
         OV(1, 0)
-        OV(2, 0)
-        OV(3, 0)
-        for i in range(4):
-            P2(i, 1)
-        QH(1, 1)
-        for i in range(4): OV(i, 1)
-        for i in range(4): ST(i, 0)
         QK(1, 2)
-        for i in range(4, 8):
-            P2(i, 0)
-        for i in range(4): ST(i, 1)
-        for i in range(4, 6):
-            OV(i, 0)
         QK(0, 2)
-        OV(6,0)
-        OS(7,0)
+        for mt in (0, 2, 3): DH("S", 1, mt)
+        P2(1, 1); P2(1, 2); P2(2, 1); P2(3, 2)
+        OV(2, 0)
+        IH("V", 1, 1)
+        OS(0, 1)
+        DH("S", 1, 1)
+        OV(2, 1)
+        for i, c in ((1, 0), (0, 0), (2, 0), (0, 1), (2, 1)):
+            ST(i, c)
+        P2(3, 1); P2(3, 0); P2(2, 2); P2(0, 2)
+        OS(1, 1)
+        OS(1, 2)
+        IH("S", 1, 0)
+        OV(3, 2)
+        OV(3, 1)
+        OV(3, 0)
+        QH(1, 1)
+        QH(1, 0)
+        OS(2, 2)
+        OV(0, 2)
+        for i, c in ((3, 2), (1, 1), (3, 1), (3, 0), (1, 2), (0, 2), (2, 2)):
+            ST(i, c)
         for i in range(4, 8):
-            P2(i, 1)
-        for i in range(4): (OV,OS)[i%2](4+i, 1)
-        for i in range(4,8): ST(i, 0)
-        for i in range(4,8): ST(i, 1)
-        for i in range(8):
-            P2(i, 2)
-        for i in range(8):
-            (OS if i in (1,3,5) else OV)(i, 2); ST(i, 2)
+            for c in range(3):
+                P2(i, c)
+            for c in range(3):
+                (OS if (i,c) in ((4,2),(6,0)) else OV)(i, c)
+            for c in range(3): ST(i, c)

@@ -1,6 +1,7 @@
 from contextlib import ExitStack
 
 import concourse.mybir as mybir
+from concourse.masks import make_identity
 
 PULSES, MONITORS, MODES, CORRECTORS = 1024, 2048, 1024, 1536
 FLOPS = 2 * PULSES * MONITORS * MODES + 2 * PULSES * MODES * CORRECTORS
@@ -15,7 +16,6 @@ E5M2 = mybir.dt.float8_e5m2_x4
 ADD = mybir.AluOpType.add
 MULT = mybir.AluOpType.mult
 SUB = mybir.AluOpType.subtract
-COPY = mybir.ActivationFunctionType.Copy
 IDENTITY = mybir.ActivationFunctionType.Identity
 
 P = 128
@@ -25,6 +25,7 @@ GROUPS = MONITORS // W
 KGROUPS = MODES // W
 HALVES = PULSES // W
 CTILES = CORRECTORS // W
+PTILES = PULSES // P
 
 
 def tile_factored_orbit_correction_e3_kernel(
@@ -34,8 +35,8 @@ def tile_factored_orbit_correction_e3_kernel(
     with ExitStack() as ctx:
         keep = ctx.enter_context(tc.tile_pool(name="keep", bufs=1))
         raws = ctx.enter_context(tc.tile_pool(name="raws", bufs=3))
-        grouped_pool = ctx.enter_context(tc.tile_pool(name="grouped", bufs=6))
-        outs = ctx.enter_context(tc.tile_pool(name="outs", bufs=12))
+        grouped_pool = ctx.enter_context(tc.tile_pool(name="grouped", bufs=5))
+        outs = ctx.enter_context(tc.tile_pool(name="outs", bufs=8))
         psum = ctx.enter_context(tc.psum_pool(name="psum", bufs=8))
         ctx.enter_context(tc.manual_schedule())
 
@@ -45,12 +46,14 @@ def tile_factored_orbit_correction_e3_kernel(
         def bank(name):
             return psum.tile([P, W], F32, name=name, tag="bank")
 
-        def four_to_a_partition(vector):
-            return vector.rearrange("(g p t) -> p g t", p=P, t=J)
-
-        tgt_raw, gain_raw, pg_raw = (kept(n, [P, 2, J], BF16) for n in ("tgt_raw", "gain_raw", "pg_raw"))
-        tgt, gain, nbias, npg = (kept(n, [P, 2, J], F32) for n in ("tgt", "gain", "nbias", "npg"))
-        nc.gpsimd.dma_start(out=pg_raw[:], in_=four_to_a_partition(pulse_gain))
+        tgt_raw, gain_raw = (kept(n, [P, KGROUPS, J], BF16) for n in ("tgt_raw", "gain_raw"))
+        tgt, gain, nbias = (kept(n, [P, KGROUPS, J], F32) for n in ("tgt", "gain", "nbias"))
+        pg_rows = kept("pg_rows", [P, P], BF16)
+        ident = kept("ident", [P, P], BF16)
+        npg = kept("npg", [P, PTILES], F32)
+        nc.gpsimd.memset(pg_rows[:], 0.0)
+        nc.gpsimd.dma_start(out=pg_rows[0:PTILES, :], in_=pulse_gain.rearrange("(i p) -> i p", p=P))
+        make_identity(nc, ident[:])
 
         g_sc = []
         for h in range(HALVES):
@@ -85,13 +88,12 @@ def tile_factored_orbit_correction_e3_kernel(
             g_w[g, 0] = words[:]
 
         def mode_vectors():
-            nc.sync.dma_start(out=tgt_raw[:], in_=four_to_a_partition(target))
-            nc.sync.dma_start(out=gain_raw[:], in_=four_to_a_partition(mode_gain))
+            nc.sync.dma_start(out=tgt_raw[:], in_=target.rearrange("(g p t) -> p g t", p=P, t=J))
+            nc.sync.dma_start(out=gain_raw[:], in_=mode_gain.rearrange("(g p t) -> p g t", p=P, t=J))
             nc.gpsimd.tensor_copy(out=tgt[:], in_=tgt_raw[:])
             nc.gpsimd.tensor_copy(out=gain[:], in_=gain_raw[:])
             nc.gpsimd.tensor_scalar(out=nbias[:], in0=tgt[:], scalar1=-1.0, scalar2=0.0, op0=MULT, op1=ADD)
             nc.gpsimd.tensor_tensor(out=nbias[:], in0=nbias[:], in1=gain[:], op=MULT)
-            nc.gpsimd.tensor_scalar(out=npg[:], in0=pg_raw[:], scalar1=-1.0, scalar2=0.0, op0=MULT, op1=ADD)
 
         load_g_words(0)
         for g in range(1, GROUPS):
@@ -101,9 +103,10 @@ def tile_factored_orbit_correction_e3_kernel(
                 ro_raw[g, mg] = raw[:, :, W * mg : W * (mg + 1)]
             if g == 1:
                 mode_vectors()
-            else:
-                load_g_words(g - 1)
-        load_g_words(GROUPS - 1)
+                load_g_words(1)
+        for g in range(2, GROUPS):
+            load_g_words(g)
+
         def kick_rows(g, c0, c1):
             return kick[W * g : W * (g + 1), W * c0 : W * c1].rearrange("(p j) n -> p j n", j=J)
 
@@ -125,14 +128,18 @@ def tile_factored_orbit_correction_e3_kernel(
             nc.sync.dma_start(out=raw[:], in_=kick_rows(g, 1, CTILES))
             for c in range(1, CTILES):
                 k_raw[g, c] = raw[:, :, W * (c - 1) : W * c]
-        def pulse_rows(array, h):
-            return array[W * h : W * (h + 1), :].rearrange("(p i) c -> p i c", i=J)
-
         sets = []
-        for h in range(HALVES):
-            st = kept(f"set{h}", [P, J, CORRECTORS], BF16)
-            nc.sync.dma_start(out=st[:], in_=pulse_rows(setting, h))
+        for i in range(PTILES):
+            st = kept(f"set{i}", [P, CORRECTORS], BF16)
+            nc.sync.dma_start(out=st[:], in_=setting[P * i : P * (i + 1), :])
             sets.append(st)
+
+        def pulse_gains():
+            columns = psum.tile([P, P], BF16, name="pg_columns", tag="bank")
+            nc.tensor.transpose(columns[:], pg_rows[:], ident[:])
+            nc.vector.tensor_scalar(
+                out=npg[:], in0=columns[:, 0:PTILES], scalar1=-1.0, scalar2=0.0, op0=MULT, op1=ADD
+            )
 
         ro_g, ro_c, ro_s = {}, {}, {}
         k_g, k_c, k_s = {}, {}, {}
@@ -157,8 +164,8 @@ def tile_factored_orbit_correction_e3_kernel(
         def deal(eng, dst, src):
             copy_on(
                 eng,
-                dst[:].rearrange("p (s m r) -> p m s r", s=4, r=J),
-                src.rearrange("p r (m s) -> p m s r", s=4),
+                dst[:].rearrange("p (s m r) -> p m r s", s=4, r=J),
+                src.rearrange("p r (m s) -> p m r s", s=4),
             )
 
         def IR(eng, g, mg):
@@ -208,7 +215,7 @@ def tile_factored_orbit_correction_e3_kernel(
 
         def IH(eng, h, mg):
             h_g[h, mg] = grouped()
-            deal(eng, h_g[h, mg], h_b[h, mg][:])
+            interleave(eng, h_g[h, mg], h_b[h, mg][:])
 
         def QH(h, mg):
             h_c[h, mg], h_s[h, mg] = quantise(f"h{h}{mg}q", E5M2, h_g[h, mg])
@@ -236,21 +243,17 @@ def tile_factored_orbit_correction_e3_kernel(
                 )
 
         def OV(i, c):
-            res[i, c] = outs.tile([P, W], F32, name="res", tag="res", align_bytes=64)
+            if i not in res:
+                res[i] = outs.tile([P, CORRECTORS], F32, name="res", tag="res", align_bytes=64)
+            cols = slice(W * c, W * (c + 1))
             nc.vector.scalar_tensor_tensor(
-                out=res[i, c][:], in0=dk[i, c][:], scalar=npg[:, i // J, i % J : i % J + 1],
-                in1=sets[i // J][:, i % J, W * c : W * (c + 1)], op0=MULT, op1=ADD,
+                out=res[i][:, cols], in0=dk[i, c][:], scalar=npg[:, i : i + 1],
+                in1=sets[i][:, cols], op0=MULT, op1=ADD,
             )
 
-        def OS(i, c):
-            res[i, c] = outs.tile([P, W], F32, name="res", tag="res", align_bytes=64)
-            nc.scalar.activation(out=res[i, c][:], in_=dk[i, c][:], func=COPY, scale=npg[:, i // J, i % J : i % J + 1])
-            nc.gpsimd.tensor_tensor(
-                out=res[i, c][:], in0=res[i, c][:], in1=sets[i // J][:, i % J, W * c : W * (c + 1)], op=ADD
-            )
-
-        def ST(i, c):
-            nc.sync.dma_start(out=pulse_rows(out, i // J)[:, i % J, W * c : W * (c + 1)], in_=res[i, c][:])
+        def ST(i, c0, c1):
+            cols = slice(W * c0, W * c1)
+            nc.sync.dma_start(out=out[P * i : P * (i + 1), cols], in_=res[i][:, cols])
 
         def p1s(g, mg):
             for t in range(J):
@@ -268,62 +271,76 @@ def tile_factored_orbit_correction_e3_kernel(
         p1s(3, 1)
         IK("S", 0, 0)
         IK("V", 1, 0)
-        for mt in (0, 3, 5, 7, 6, 4):
+        for mt in range(6):
             DH("S", 0, mt)
-        DH("V", 0, 2)
-        QK(0, 0)
-        DH("V", 0, 1)
-        for mt in (4, 5, 6, 7, 0, 2, 3):
+        DH("V", 0, 6)
+        DH("V", 0, 7)
+        pulse_gains()
+        for mt in range(5):
             for g in range(4):
                 P1(1, mt, g)
+        QK(0, 0)
         QK(1, 0)
         IH("V", 0, 0)
         IH("V", 0, 1)
-        DH("S", 1, 4)
         QH(0, 0)
         QH(0, 1)
+        DH("S", 1, 0)
+        DH("S", 1, 1)
         IK("S", 0, 1)
-        IK("V", 1, 1)
-        DH("S", 1, 6)
-        DH("V", 1, 5)
+        DH("S", 1, 2)
+        DH("S", 1, 3)
         for i in range(3):
             P2(i, 0)
-        QK(0, 1)
-        QK(1, 1)
-        P2(0, 1)
+        for mt in (5, 6, 7):
+            for g in range(4):
+                P1(1, mt, g)
+        IK("V", 1, 1)
         IK("S", 1, 2)
         IK("V", 0, 2)
-        DH("S", 1, 7)
-        for g in range(4): P1(1, 1, g)
-        OS(0, 0)
+        QK(0, 1)
+        OV(0, 0)
         OV(1, 0)
-        QK(1, 2)
-        QK(0, 2)
-        for mt in (0, 2, 3): DH("S", 1, mt)
-        P2(1, 1); P2(1, 2); P2(2, 1); P2(3, 2)
+        QK(1, 1)
         OV(2, 0)
-        IH("V", 1, 1)
-        OS(0, 1)
-        DH("S", 1, 1)
+        DH("S", 1, 4)
+        P2(0, 1)
+        P2(1, 1)
+        P2(2, 1)
+        P2(3, 0)
+        P2(3, 1)
+        DH("S", 1, 5)
+        DH("S", 1, 6)
+        DH("S", 1, 7)
+        for i in range(3):
+            ST(i, 0, 1)
+        QK(0, 2)
+        OV(0, 1)
+        QK(1, 2)
+        OV(1, 1)
         OV(2, 1)
-        for i, c in ((1, 0), (0, 0), (2, 0), (0, 1), (2, 1)):
-            ST(i, c)
-        P2(3, 1); P2(3, 0); P2(2, 2); P2(0, 2)
-        OS(1, 1)
-        OS(1, 2)
         IH("S", 1, 0)
-        OV(3, 2)
-        OV(3, 1)
+        IH("S", 1, 1)
+        for i in range(4):
+            P2(i, 2)
+        for i in range(3):
+            ST(i, 1, 2)
         OV(3, 0)
-        QH(1, 1)
+        OV(3, 1)
+        ST(3, 0, 2)
         QH(1, 0)
-        OS(2, 2)
         OV(0, 2)
-        for i, c in ((3, 2), (1, 1), (3, 1), (3, 0), (1, 2), (0, 2), (2, 2)):
-            ST(i, c)
+        OV(1, 2)
+        QH(1, 1)
+        OV(2, 2)
+        OV(3, 2)
+        for i in range(4):
+            ST(i, 2, 3)
         for i in range(4, 8):
             for c in range(3):
                 P2(i, c)
-            for c in range(3):
-                (OS if (i,c) in ((4,2),(6,0)) else OV)(i, c)
-            for c in range(3): ST(i, c)
+            OV(i, 0)
+            OV(i, 1)
+            ST(i, 0, 2)
+            OV(i, 2)
+            ST(i, 2, 3)

from contextlib import ExitStack

import concourse.mybir as mybir
from concourse.masks import make_identity

PULSES, MONITORS, MODES, CORRECTORS = 1024, 2048, 1024, 1536
FLOPS = 2 * PULSES * MONITORS * MODES + 2 * PULSES * MODES * CORRECTORS

F32 = mybir.dt.float32
BF16 = mybir.dt.bfloat16
U32 = mybir.dt.uint32
I32 = mybir.dt.int32
U8 = mybir.dt.uint8
E4M3 = mybir.dt.float8_e4m3fn_x4
E5M2 = mybir.dt.float8_e5m2_x4
ADD = mybir.AluOpType.add
MULT = mybir.AluOpType.mult
SUB = mybir.AluOpType.subtract
IDENTITY = mybir.ActivationFunctionType.Identity

P = 128
J = 4
W = 512
GROUPS = MONITORS // W
KGROUPS = MODES // W
HALVES = PULSES // W
CTILES = CORRECTORS // W
PTILES = PULSES // P


def tile_factored_orbit_correction_e3_kernel(
    tc, g_words, g_scales, readout, target, mode_gain, kick, pulse_gain, setting, out
):
    nc = tc.nc
    with ExitStack() as ctx:
        keep = ctx.enter_context(tc.tile_pool(name="keep", bufs=1))
        raws = ctx.enter_context(tc.tile_pool(name="raws", bufs=3))
        grouped_pool = ctx.enter_context(tc.tile_pool(name="grouped", bufs=5))
        outs = ctx.enter_context(tc.tile_pool(name="outs", bufs=8))
        psum = ctx.enter_context(tc.psum_pool(name="psum", bufs=8))
        ctx.enter_context(tc.manual_schedule())

        def kept(name, shape, dtype):
            return keep.tile(shape, dtype, name=name, tag=name, align_bytes=64)

        def bank(name):
            return psum.tile([P, W], F32, name=name, tag="bank")

        tgt_raw, gain_raw = (kept(n, [P, KGROUPS, J], BF16) for n in ("tgt_raw", "gain_raw"))
        tgt, gain, nbias = (kept(n, [P, KGROUPS, J], F32) for n in ("tgt", "gain", "nbias"))
        pg_rows = kept("pg_rows", [P, P], BF16)
        ident = kept("ident", [P, P], BF16)
        npg = kept("npg", [P, PTILES], F32)
        nc.gpsimd.memset(pg_rows[:], 0.0)
        nc.gpsimd.dma_start(out=pg_rows[0:PTILES, :], in_=pulse_gain.rearrange("(i p) -> i p", p=P))
        make_identity(nc, ident[:])

        g_sc = []
        for h in range(HALVES):
            plane = kept(f"g_sc{h}", [P, GROUPS, W], U8)
            nc.vector.memset(plane[:].rearrange("p g n -> p (g n)").bitcast(I32), 0)
            g_sc.append(plane)

        def load_g_scales(h):
            for q in range(4):
                nc.sync.dma_start(
                    out=g_sc[h][32 * q : 32 * q + 4].bitcast(I32),
                    in_=g_scales[:, 4 * q : 4 * q + 4, W * h : W * (h + 1)].rearrange("g r n -> r g n").bitcast(I32),
                )

        def ro_rows(g):
            return readout[W * g : W * (g + 1), :].rearrange("(p j) w -> p j w", j=J)

        ro_raw = {}
        g_w = {}
        for mg in range(KGROUPS):
            raw = kept(f"ro0_{mg}", [P, J, W], BF16)
            nc.sync.dma_start(out=raw[:], in_=ro_rows(0)[:, :, W * mg : W * (mg + 1)])
            ro_raw[0, mg] = raw[:]
        load_g_scales(0)

        def load_g_words(g):
            words = kept(f"gw_{g}", [P, W], U32)
            nc.sync.dma_start(
                out=words[:].bitcast(I32),
                in_=g_words[g, :, 0:W, :].rearrange("p n t -> p (n t)").bitcast(I32),
            )
            g_w[g, 0] = words[:]

        def mode_vectors():
            nc.sync.dma_start(out=tgt_raw[:], in_=target.rearrange("(g p t) -> p g t", p=P, t=J))
            nc.sync.dma_start(out=gain_raw[:], in_=mode_gain.rearrange("(g p t) -> p g t", p=P, t=J))
            nc.gpsimd.tensor_copy(out=tgt[:], in_=tgt_raw[:])
            nc.gpsimd.tensor_copy(out=gain[:], in_=gain_raw[:])
            nc.gpsimd.tensor_scalar(out=nbias[:], in0=tgt[:], scalar1=-1.0, scalar2=0.0, op0=MULT, op1=ADD)
            nc.gpsimd.tensor_tensor(out=nbias[:], in0=nbias[:], in1=gain[:], op=MULT)

        load_g_words(0)
        for g in range(1, GROUPS):
            raw = raws.tile([P, J, MODES], BF16, name="ro_raw", tag="ro_raw", align_bytes=64)
            nc.sync.dma_start(out=raw[:], in_=ro_rows(g))
            for mg in range(KGROUPS):
                ro_raw[g, mg] = raw[:, :, W * mg : W * (mg + 1)]
            if g == 1:
                mode_vectors()
                load_g_words(1)
        for g in range(2, GROUPS):
            load_g_words(g)

        def kick_rows(g, c0, c1):
            return kick[W * g : W * (g + 1), W * c0 : W * c1].rearrange("(p j) n -> p j n", j=J)

        k_raw = {}
        for g in range(KGROUPS):
            raw = kept(f"k_raw{g}0", [P, J, W], BF16)
            nc.sync.dma_start(out=raw[:], in_=kick_rows(g, 0, 1))
            k_raw[g, 0] = raw[:]
        load_g_scales(1)
        words1 = kept("gw_half1", [P, GROUPS, W], U32)
        nc.sync.dma_start(
            out=words1[:].bitcast(I32),
            in_=g_words[:, :, W : 2 * W, :].rearrange("g p n t -> p g (n t)").bitcast(I32),
        )
        for g in range(GROUPS):
            g_w[g, 1] = words1[:, g, :]
        for g in range(KGROUPS):
            raw = kept(f"k_raw{g}r", [P, J, 2 * W], BF16)
            nc.sync.dma_start(out=raw[:], in_=kick_rows(g, 1, CTILES))
            for c in range(1, CTILES):
                k_raw[g, c] = raw[:, :, W * (c - 1) : W * c]
        sets = []
        for i in range(PTILES):
            st = kept(f"set{i}", [P, CORRECTORS], BF16)
            nc.sync.dma_start(out=st[:], in_=setting[P * i : P * (i + 1), :])
            sets.append(st)

        def pulse_gains():
            columns = psum.tile([P, P], BF16, name="pg_columns", tag="bank")
            nc.tensor.transpose(columns[:], pg_rows[:], ident[:])
            nc.vector.tensor_scalar(
                out=npg[:], in0=columns[:, 0:PTILES], scalar1=-1.0, scalar2=0.0, op0=MULT, op1=ADD
            )

        ro_g, ro_c, ro_s = {}, {}, {}
        k_g, k_c, k_s = {}, {}, {}
        h_b, h_g, h_c, h_s = {}, {}, {}, {}
        amp, dk, res = {}, {}, {}

        def grouped():
            return grouped_pool.tile([P, J * W], BF16, name="grp", tag="grp", align_bytes=64)

        def copy_on(eng, dst, src):
            if eng == "V":
                nc.vector.tensor_copy(out=dst, in_=src)
            else:
                nc.scalar.copy(out=dst, in_=src)

        def quantise(name, fmt, src):
            codes = kept(name + "_c", [P, W], U32)
            scales = kept(name + "_s", [P, W], U8)
            nc.vector.quantize_mx(out=codes[:].bitcast(fmt), scales=scales[:], in_=src[:])
            return codes, scales

        def deal(eng, dst, src):
            copy_on(
                eng,
                dst[:].rearrange("p (s m r) -> p m r s", s=4, r=J),
                src.rearrange("p r (m s) -> p m r s", s=4),
            )

        def IR(eng, g, mg):
            ro_g[g, mg] = grouped()
            deal(eng, ro_g[g, mg], ro_raw[g, mg])

        def QR(g, mg):
            ro_c[g, mg], ro_s[g, mg] = quantise(f"ro{g}{mg}", E4M3, ro_g[g, mg])

        def P1(h, mt, g):
            if g == 0:
                amp[h, mt] = bank(f"amp{h}{mt}")
            mg, t = divmod(mt, J)
            cols = slice(P * t, P * (t + 1))
            nc.tensor.matmul_mx(
                out=amp[h, mt][:],
                lhsT=ro_c[g, mg][:, cols].bitcast(E4M3),
                lhsT_scale=ro_s[g, mg][:, cols],
                rhs=g_w[g, h].bitcast(E5M2),
                rhs_scale=g_sc[h][:, g, :],
                start=(g == 0),
                stop=(g == GROUPS - 1),
            )

        def DH(eng, h, mt):
            mg, t = divmod(mt, J)
            if (h, mg) not in h_b:
                h_b[h, mg] = kept(f"h{h}{mg}", [P, J, W], BF16)
            dst = h_b[h, mg][:, t, :]
            if eng == "V":
                nc.vector.tensor_scalar(
                    out=dst, in0=amp[h, mt][:], scalar1=tgt[:, mg, t : t + 1],
                    scalar2=gain[:, mg, t : t + 1], op0=SUB, op1=MULT,
                )
            else:
                nc.scalar.activation(
                    out=dst, in_=amp[h, mt][:], func=IDENTITY,
                    scale=gain[:, mg, t : t + 1], bias=nbias[:, mg, t : t + 1],
                )

        def interleave(eng, dst, src):
            copy_on(
                eng,
                dst[:].rearrange("p (c i t) -> p c t i", i=4, t=J),
                src.rearrange("p t (c i) -> p c t i", i=4),
            )

        def IH(eng, h, mg):
            h_g[h, mg] = grouped()
            interleave(eng, h_g[h, mg], h_b[h, mg][:])

        def QH(h, mg):
            h_c[h, mg], h_s[h, mg] = quantise(f"h{h}{mg}q", E5M2, h_g[h, mg])

        def IK(eng, g, c):
            k_g[g, c] = grouped()
            interleave(eng, k_g[g, c], k_raw[g, c])

        def QK(g, c):
            k_c[g, c], k_s[g, c] = quantise(f"k{g}{c}", E4M3, k_g[g, c])

        def P2(i, c):
            dk[i, c] = bank(f"dk{i}{c}")
            h, r = divmod(i, W // P)
            cols = slice(P * r, P * (r + 1))
            for g in range(KGROUPS):
                nc.tensor.matmul_mx(
                    out=dk[i, c][:],
                    lhsT=h_c[h, g][:, cols].bitcast(E5M2),
                    lhsT_scale=h_s[h, g][:, cols],
                    rhs=k_c[g, c][:].bitcast(E4M3),
                    rhs_scale=k_s[g, c][:],
                    start=(g == 0),
                    stop=(g == KGROUPS - 1),
                )

        def OV(i, c):
            if i not in res:
                res[i] = outs.tile([P, CORRECTORS], F32, name="res", tag="res", align_bytes=64)
            cols = slice(W * c, W * (c + 1))
            nc.vector.scalar_tensor_tensor(
                out=res[i][:, cols], in0=dk[i, c][:], scalar=npg[:, i : i + 1],
                in1=sets[i][:, cols], op0=MULT, op1=ADD,
            )

        def ST(i, c0, c1):
            cols = slice(W * c0, W * c1)
            nc.sync.dma_start(out=out[P * i : P * (i + 1), cols], in_=res[i][:, cols])

        def p1s(g, mg):
            for t in range(J):
                P1(0, J * mg + t, g)

        for g in range(4):
            IR("V", g, 0)
            IR("S", g, 1)
            if g:
                QR(g - 1, 1)
                p1s(g - 1, 1)
            QR(g, 0)
            p1s(g, 0)
        QR(3, 1)
        p1s(3, 1)
        IK("S", 0, 0)
        IK("V", 1, 0)
        for mt in range(6):
            DH("S", 0, mt)
        DH("V", 0, 6)
        DH("V", 0, 7)
        pulse_gains()
        for mt in range(5):
            for g in range(4):
                P1(1, mt, g)
        QK(0, 0)
        QK(1, 0)
        IH("V", 0, 0)
        IH("V", 0, 1)
        QH(0, 0)
        QH(0, 1)
        DH("S", 1, 0)
        DH("S", 1, 1)
        IK("S", 0, 1)
        DH("S", 1, 2)
        DH("S", 1, 3)
        for i in range(3):
            P2(i, 0)
        for mt in (5, 6, 7):
            for g in range(4):
                P1(1, mt, g)
        IK("V", 1, 1)
        IK("S", 1, 2)
        IK("V", 0, 2)
        QK(0, 1)
        OV(0, 0)
        OV(1, 0)
        QK(1, 1)
        OV(2, 0)
        DH("S", 1, 4)
        P2(0, 1)
        P2(1, 1)
        P2(2, 1)
        P2(3, 0)
        P2(3, 1)
        DH("S", 1, 5)
        DH("S", 1, 6)
        DH("S", 1, 7)
        for i in range(3):
            ST(i, 0, 1)
        QK(0, 2)
        OV(0, 1)
        QK(1, 2)
        OV(1, 1)
        OV(2, 1)
        IH("S", 1, 0)
        IH("S", 1, 1)
        for i in range(4):
            P2(i, 2)
        for i in range(3):
            ST(i, 1, 2)
        OV(3, 0)
        OV(3, 1)
        ST(3, 0, 2)
        QH(1, 0)
        OV(0, 2)
        OV(1, 2)
        QH(1, 1)
        OV(2, 2)
        OV(3, 2)
        for i in range(4):
            ST(i, 2, 3)
        for i in range(4, 8):
            for c in range(3):
                P2(i, c)
            OV(i, 0)
            OV(i, 1)
            ST(i, 0, 2)
            OV(i, 2)
            ST(i, 2, 3)
